import numpy as np, ml_dtypes
CORES = [8,80,112,136,208,240,264,336,368,392,464,496]
N = 12
DEG, TK, TIMES = 12, 128, 2
MASK = [[0,1,2,3,4,5,6,7,8,9,10,11],[0,1,2,3,4,5,6,7,8,9,10,11],[0,1,2,3,4,5,6,7,8,9,10,11],[0,1,2,3,4,5,6,7,8,9,10,11],[0,1,2,3,4,5,6,7,8,9,10,11],[0,1,2,3,4,5,6,7,8,9,10,11],[0,1,2,3,4,5,6,7,8,9,10,11],[0,1,2,3,4,5,6,7,8,9,10,11],[0,1,2,3,4,5,6,7,8,9,10,11],[0,1,2,3,4,5,6,7,8,9,10,11],[0,1,2,3,4,5,6,7,8,9,10,11],[0,1,2,3,4,5,6,7,8,9,10,11]]
def setup_inputs(rng):
    return {"x": rng.standard_normal((N, 128, TK), dtype=np.float32).astype(ml_dtypes.bfloat16), "w": (rng.standard_normal((N, 128, DEG * 128), dtype=np.float32) / np.float32(np.sqrt(128 * DEG / 2))).astype(ml_dtypes.bfloat16)}
def setup_inputs_big(rng):
    d = setup_inputs(rng)
    for k in ("x",): d[k] = (d[k].astype(np.float32) * 1048576.0).astype(d[k].dtype)
    return d
def setup_inputs_small(rng):
    d = setup_inputs(rng)
    for k in ("x",): d[k] = (d[k].astype(np.float32) * (1 / 1048576.0)).astype(d[k].dtype)
    return d
def setup_inputs_apart(rng):
    d = setup_inputs(rng)
    f = (10.0 ** rng.permutation(np.linspace(-1.5, 1.5, N))).astype(np.float32).reshape(N, 1, 1)
    for k in ("x",): d[k] = (d[k].astype(np.float32) * f).astype(d[k].dtype)
    return d
def reference(x, w):
    X, W = x.astype(np.float64), w.astype(np.float64)
    h = list(X)
    for _ in range(TIMES):
        h = [np.maximum(sum(W[r][:, 128 * i:128 * i + 128].T @ h[j] for i, j in enumerate(MASK[r])), 0.0) for r in range(N)]
    return {"y": np.stack(h).astype(ml_dtypes.bfloat16)}

from concourse.bass import DstId, RemoteDMATransfer
from concourse.mybir import AluOpType

N, TK, TIMES, NCORES = 12, 128, 2, 512

SCRATCH = {
    "h0": ("sbuf", [128, N * TK], "bfloat16"),
    "h1": ("sbuf", [128, N * TK], "bfloat16"),
    "wsb": ("sbuf", [128, N * TK], "bfloat16"),
    "zero": ("sbuf", [128, TK], "float32"),
    "yout": ("sbuf", [128, TK], "bfloat16"),
    "acc0": ("psum", [128, 512], "float32"),
    "acc1": ("psum", [128, 512], "float32"),
}
SEMAPHORES = ["a%d_%d" % (k, j) for k in range(TIMES) for j in range(N)] + ["wl", "zs", "mm0", "mm1", "yr", "yd", "sent"]

_PLANS = {}
HOP, TILE = 2.5, 1.0


def _count(mask):
    return sum(1 for b in range(16) if (mask >> b) & 1)


def _rot(lst, start):
    return lst[start:] + lst[:start]


def _split(lst, parts):
    out, i = [], 0
    for p in range(parts):
        n = (len(lst) - i + (parts - p) - 1) // (parts - p)
        out.append(lst[i:i + n])
        i += n
    return [o for o in out if o]


def _plan(cores, mask_table, topo):
    allc = range(NCORES)
    place = lambda c: (topo.host(c), topo.chip(c))
    rack = lambda c: topo.rack(topo.host(c))

    def owners(chip_cores):
        mate = [k for k in allc if topo.mates(chip_cores[0], k)]
        return [c for c in chip_cores if mate and topo.may_write(c, mate[0])]

    sends, recv, eta = {}, {}, {}

    def emit(src, j, t0, transfers):
        transfers = [(m, d) for m, d in transfers if d]
        if not transfers:
            return
        sends[src] = (j, transfers)
        for m, dsts in transfers:
            for p, d in enumerate(dsts):
                recv[(d, j)] = _count(m)
                eta[(d, j)] = t0 + (p + 1) * TILE

    for j, s in enumerate(cores):
        dests = [cores[r] for r in range(len(cores)) if r != j and j in mask_table[r]]
        home = [c for c in allc if place(c) == place(s) and c != s and c not in cores]
        twin = [c for c in allc if rack(c) != rack(s) and topo.chip(c) == topo.chip(s) and topo.may_write(s, c)]
        ring_n = [c for c in cores if rack(c) == rack(s)]
        ring_f = [c for c in cores if rack(c) != rack(s)]
        near = [c for c in _rot(ring_n, ring_n.index(s)) if c in dests]
        anchor = [i for i, c in enumerate(ring_f) if c in twin]
        far = [c for c in _rot(ring_f, anchor[0] if anchor else 0) if c in dests]
        straight = [c for c in near if topo.may_write(s, c)]
        across = [c for c in near if not topo.may_write(s, c)]
        cable = [c for c in far if c in twin]
        beyond = [c for c in far if c not in twin]
        nh = [c for c in owners(home) if topo.die(c) == topo.die(s)]
        fh = [c for c in owners(twin) if topo.die(c) != topo.die(s) and c not in cores]
        near_parts = _split(across, min(len(nh), (len(across) + 1) // 2))
        far_parts = _split(beyond, min(len(fh), 2))
        nh, fh = nh[:len(near_parts)], fh[:len(far_parts)]
        off = topo.mask(s, twin[0])
        on = topo.mask(s, home[0]) & ~off
        emit(s, j, 0.0, [(off, fh + straight + cable), (on, nh)])
        for h, part in list(zip(nh, near_parts)) + list(zip(fh, far_parts)):
            m = topo.mask(h, part[0])
            for d in part:
                m &= topo.mask(h, d)
            emit(h, j, eta[(h, j)] + HOP, [(m, part)])
    return sends, recv, eta


def _send(g, core, T, topo, k, j, transfers):
    blk = T["h%d" % k][:, j * TK:(j + 1) * TK]
    trs, n = [], 0
    for m, dsts in transfers:
        ids = []
        for d in dsts:
            rid, pid = topo.addr(d, core)
            ids.append(DstId(rid=rid, pnc=pid))
        trs.append(RemoteDMATransfer(dst_ids=ids, dma_engine_mask=m, remote_sem=T.sem["a%d_%d" % (k, j)],
                                     srcs=[blk], dsts=[blk for _ in dsts], alu_op=0))
        n += _count(m)
    g.remote_dma_fused(trs, local_sem=T.sem.sent)
    return n


def rank_program(g, core, T, topo):
    cores = list(T.cores)
    table = T.tables["MASK"]
    key = tuple(cores)
    if key not in _PLANS:
        _PLANS[key] = _plan(cores, table, topo)
    sends, recv, eta = _PLANS[key]
    rank = T.rank_of(core)

    if rank is None:
        if core not in sends:
            return
        j, transfers = sends[core]
        left = 0
        for k in range(TIMES):
            g.wait_ge(T.sem["a%d_%d" % (k, j)], recv[(core, j)])
            left += _send(g, core, T, topo, k, j, transfers)
        g.wait_ge(T.sem.sent, left)
        return

    own = slice(rank * TK, (rank + 1) * TK)
    g.sync.dma_start(T.h0[:, own], T.x[:, :]).then_inc(T.sem["a0_%d" % rank], 16)
    g.sync.dma_start(T.wsb[:, :], T.w[:, :]).then_inc(T.sem.wl, 16)
    g.vector.memset(T.zero[:, :], 0.0).then_inc(T.sem.zs, 1)
    g.vector.wait_ge(T.sem.zs, 1)

    level = [{rank: 16}, {rank: 1}]
    when = {rank: -1.0}
    for j in range(len(cores)):
        if (core, j) in recv:
            level[0][j] = level[1][j] = recv[(core, j)]
            when[j] = eta[(core, j)]
    order = sorted(range(len(table[rank])), key=lambda i: (when[table[rank][i]], i))

    left = 0
    for k in range(TIMES):
        if core in sends:
            g.wait_ge(T.sem["a%d_%d" % (k, rank)], level[k][rank])
            left += _send(g, core, T, topo, k, rank, sends[core][1])
    if left:
        g.wait_ge(T.sem.sent, left)

    g.tensor.wait_ge(T.sem.wl, 16)
    for k in range(TIMES):
        acc = T["acc%d" % k][:, 0:TK]
        for n, i in enumerate(order):
            j = table[rank][i]
            g.tensor.wait_ge(T.sem["a%d_%d" % (k, j)], level[k][j])
            mm = g.tensor.matmul(acc, T.wsb[:, i * TK:(i + 1) * TK], T["h%d" % k][:, j * TK:(j + 1) * TK],
                                 n == 0, n == len(order) - 1)
        mm.then_inc(T.sem["mm%d" % k], 1)

    g.vector.wait_ge(T.sem.mm0, 1)
    g.vector.tensor_tensor(T.h1[:, own], T.acc0[:, 0:TK], T.zero[:, :], AluOpType.max).then_inc(T.sem["a1_%d" % rank], 1)
    g.vector.wait_ge(T.sem.mm1, 1)
    g.vector.tensor_tensor(T.yout[:, :], T.acc1[:, 0:TK], T.zero[:, :], AluOpType.max).then_inc(T.sem.yr, 1)
    g.sync.wait_ge(T.sem.yr, 1)
    g.sync.dma_start(T.y[:, :], T.yout[:, :]).then_inc(T.sem.yd, 16)
    g.sync.wait_ge(T.sem.yd, 16)
